import numpy as np
import ml_dtypes


def mxq(x, axis, fmt="e4m3"):
    dtype, down = {"e4m3": (ml_dtypes.float8_e4m3fn, 7), "e5m2": (ml_dtypes.float8_e5m2, 14)}[fmt]
    v = np.moveaxis(np.asarray(x, np.float32).astype(ml_dtypes.bfloat16).astype(np.float64), axis, -1)
    blocks = v.reshape(v.shape[:-1] + (-1, 32))
    amax = np.abs(blocks).max(-1, keepdims=True)
    byte = np.maximum(np.where(amax > 0, np.frexp(amax)[1] - 1 + 127, 0) - down, 1)
    scale = np.exp2(byte - 127.0)
    codes = (blocks / scale).astype(np.float32).astype(dtype).astype(np.float64)
    return np.moveaxis((codes * scale).reshape(v.shape), -1, axis)


WIDE = False


def mx_kscale(k):
    if not WIDE:
        return np.ones(k)
    levels = np.array([10, -10, 5, -5, 0])
    if k % 512:
        return np.exp2(np.random.permutation(np.resize(levels, k // 32))).repeat(32)
    a = np.empty((k // 512, 16))
    for p in range(k // 512):
        a[p, :8] = np.random.permutation(np.resize(levels, 8))
        for g in range(8):
            far = levels[np.abs(levels - a[p, g]) >= 10]
            a[p, g + 8] = far[np.random.randint(len(far))]
    return np.exp2(a.ravel()).repeat(32)


def f64(x):
    return np.asarray(x).astype(np.float64)


def striped(idx):
    return np.tile(np.asarray(idx).reshape(-1, 16).T, (8, 1)).astype(np.uint16)


def unstriped(offs):
    return offs[:16].T.reshape(-1).astype(np.int64)


E2M1 = np.array([0.0, 0.5, 1.0, 1.5, 2.0, 3.0, 4.0, 6.0, -0.0, -0.5, -1.0, -1.5, -2.0, -3.0, -4.0, -6.0])


def pack_weight(w, fmt):
    k, n = w.shape
    w = f64(np.asarray(w, np.float32).astype(ml_dtypes.bfloat16)).reshape(k // 32, 32, n)
    amax = np.abs(w).max(1)
    if fmt == "e4m3":
        byte = np.frexp(amax)[1] - 1 + 127 - 7
    else:
        mant, ex = np.frexp(amax / 6.0)
        byte = np.where(mant > 0.5, ex, ex - 1) + 127
    byte = np.clip(np.where(amax > 0, byte, 1), 1, 254)
    scaled = (w * np.exp2(127.0 - byte)[:, None, :]).reshape(k, n).astype(np.float32)
    by_word = np.ascontiguousarray(scaled.reshape(k // 512, 128, 4, n).transpose(0, 1, 3, 2))
    if fmt == "e4m3":
        words = by_word.astype(ml_dtypes.float8_e4m3fn).view(np.uint8)
    else:
        c = by_word.astype(ml_dtypes.float4_e2m1fn).view(np.uint8) & 0xF
        words = (c[..., 0::2] | (c[..., 1::2] << 4)).reshape(k // 512, 128, 2 * n)
    return np.ascontiguousarray(words), np.ascontiguousarray(byte.astype(np.uint8).reshape(k // 512, 16, n))


def unpack_weight(words, scales, fmt):
    g, _, n = scales.shape
    words = np.ascontiguousarray(words).reshape(g, 128, n, -1)
    if fmt == "e4m3":
        vals = words.view(ml_dtypes.float8_e4m3fn).astype(np.float64)
    else:
        nib = np.empty((g, 128, n, 4), np.uint8)
        nib[..., 0::2] = words & 0xF
        nib[..., 1::2] = words >> 4
        vals = E2M1[nib]
    vals = vals * np.repeat(np.exp2(scales.astype(np.float64) - 127.0), 8, axis=1)[..., None]
    return vals.transpose(0, 1, 3, 2).reshape(g * 512, n)


def sigmoid(v):
    return 1.0 / (1.0 + np.exp(-v))


D, E, T, I, Q = 512, 512, 2048, 512, 128


def setup_inputs():
    n = np.random.standard_normal
    idx = np.random.permutation(T)[:I]
    fd = mx_kscale(D)
    fe = mx_kscale(E)
    keysp = pack_weight(n((D, T)) / fd[:, None], "e4m3")
    valsp = pack_weight(n((E, T)) / fe[:, None], "e4m3")
    return {
        "query": (n((D, Q)) * 0.8 / np.sqrt(D) * fd[:, None]).astype(np.float32),
        "keys_words": keysp[0],
        "keys_scales": keysp[1],
        "share": (np.random.uniform(0.2, 0.8, (Q, 1))).astype(np.float32),
        "gout": (n((E, Q)) * 1 / np.sqrt(E) * fe[:, None]).astype(np.float32),
        "vals_words": valsp[0],
        "vals_scales": valsp[1],
        "old": (0.5 * n((Q, T))).astype(np.float32),
        "offs": striped(idx),
    }


def reference(query, keys_words, keys_scales, share, gout, vals_words, vals_scales, old, offs):
    idx = unstriped(offs)
    keysu = unpack_weight(keys_words, keys_scales, "e4m3")
    valsu = unpack_weight(vals_words, vals_scales, "e4m3")
    queryq = mxq(f64(query), 0, "e4m3")
    keysidxg = keysu[:, idx]
    a = queryq.T @ keysidxg
    e0 = np.exp(a)
    s0 = sigmoid(a)
    p = e0 * f64(share) + s0 * (1.0 - f64(share)) * 3.0
    z = np.sum(p, axis=1, keepdims=True)
    goutq = mxq(f64(gout), 0, "e4m3")
    valsidxg = valsu[:, idx]
    c0 = goutq.T @ valsidxg
    dz = np.sum(c0 * p / np.square(z) * (-1.0), axis=1, keepdims=True)
    dp = c0 / z + dz
    ds0 = dp * 3.0 * (1.0 - f64(share))
    de0 = dp * f64(share)
    da = ds0 * s0 * (1.0 - s0) + de0 * e0
    gs = da * 512.0
    gf = np.zeros((Q, T))
    gf[:, idx] = gs
    y = f64(old) + gf
    return y

@@ -1,0 +1,123 @@
+from contextlib import ExitStack
+
+import concourse.mybir as mybir
+
+D, E, T, SLOTS, Q = 512, 512, 2048, 512, 128
+FLOPS = 2 * Q * SLOTS * (D + E)
+
+F32 = mybir.dt.float32
+BF16 = mybir.dt.bfloat16
+I32 = mybir.dt.int32
+U32 = mybir.dt.uint32
+U16 = mybir.dt.uint16
+U8 = mybir.dt.uint8
+FP8X4 = mybir.dt.float8_e4m3fn_x4
+ALU = mybir.AluOpType
+ACT = mybir.ActivationFunctionType
+
+P = 128
+PACK = 4
+HALF = SLOTS // 2
+OUT_CHUNK = 512
+
+
+def tile_attend_bmixedparts_s_kernel(tc, query, keys_words, keys_scales, share, gout, vals_words, vals_scales, old, offs, out):
+    nc = tc.nc
+    with ExitStack() as ctx:
+        sb = ctx.enter_context(tc.tile_pool(name="sb", bufs=1))
+        ps = ctx.enter_context(tc.psum_pool(name="ps", bufs=1))
+
+        offsets = sb.tile([P, SLOTS // 16], U16, name="offsets")
+        nc.sync.dma_start(offsets[:], offs)
+
+        k_bytes = sb.tile([P, T], U8, name="k_bytes", tag="k_bytes_then_kw", align_bytes=64)
+        v_bytes = sb.tile([P, T], U8, name="v_bytes", tag="v_bytes_then_vw", align_bytes=64)
+        nc.vector.memset(k_bytes[:].bitcast(I32), 0)
+        nc.vector.memset(v_bytes[:].bitcast(I32), 0)
+
+        q_raw = sb.tile([P, PACK, Q], F32, name="q_raw", tag="raw")
+        nc.scalar.dma_start(q_raw[:], query.rearrange("(p j) q -> p j q", j=PACK))
+        k_words = sb.tile([P, T], U32, name="k_words", tag="keys_then_old")
+        nc.sync.dma_start(k_words[:].bitcast(I32), keys_words[0].rearrange("p t r -> p (t r)").bitcast(I32))
+        for quad in range(4):
+            nc.scalar.dma_start(k_bytes[32 * quad : 32 * quad + 4, :].bitcast(I32), keys_scales[0, 4 * quad : 4 * quad + 4, :].bitcast(I32))
+        mix_exp = sb.tile([P, 1], F32, name="mix_exp")
+        nc.gpsimd.dma_start(mix_exp[:], share)
+        v_words = sb.tile([P, T], U32, name="v_words", tag="v_words_then_part_exp")
+        nc.sync.dma_start(v_words[:].bitcast(I32), vals_words[0].rearrange("p t r -> p (t r)").bitcast(I32))
+        for quad in range(4):
+            nc.gpsimd.dma_start(v_bytes[32 * quad : 32 * quad + 4, :].bitcast(I32), vals_scales[0, 4 * quad : 4 * quad + 4, :].bitcast(I32))
+
+        placed = sb.tile([P, T], F32, name="placed")
+        nc.vector.memset(placed[:, : T // 2 - 1], 0.0)
+        nc.vector.memset(placed[:, T // 2 - 1 :], 0.0)
+
+        mix_sig = sb.tile([P, 1], F32, name="mix_sig")
+        mix_sig_neg = sb.tile([P, 1], F32, name="mix_sig_neg")
+        nc.scalar.activation(mix_sig[:], mix_exp[:], ACT.Copy, bias=3.0, scale=-3.0)
+        nc.scalar.activation(mix_sig_neg[:], mix_exp[:], ACT.Copy, bias=-3.0, scale=3.0)
+
+        q_bf = sb.tile([P, Q, PACK], BF16, name="q_bf", align_bytes=64)
+        nc.vector.tensor_copy(q_bf[:], q_raw[:].rearrange("p j q -> p q j"))
+        ks = sb.tile([P, SLOTS], U8, name="ks", align_bytes=64)
+        nc.vector.tensor_copy(ks[:], k_bytes[:].indirect(offsets[:]))
+        q_codes = sb.tile([P, Q], U32, name="q_codes", align_bytes=64)
+        q_scales = sb.tile([P, Q], U8, name="q_scales", align_bytes=64)
+        nc.vector.quantize_mx(out=q_codes[:].bitcast(FP8X4), scales=q_scales[:], in_=q_bf[:].rearrange("p q j -> p (q j)"))
+
+        g_raw = sb.tile([P, PACK, Q], F32, name="g_raw", tag="raw")
+        nc.scalar.dma_start(g_raw[:], gout.rearrange("(p j) q -> p j q", j=PACK))
+        g_bf = sb.tile([P, Q, PACK], BF16, name="g_bf", align_bytes=64)
+        nc.scalar.copy(g_bf[:], g_raw[:].rearrange("p j q -> p q j"))
+
+        e0 = sb.tile([P, SLOTS], F32, name="e0")
+        s0 = sb.tile([P, SLOTS], F32, name="s0")
+        scores = []
+        kw = sb.tile([P, SLOTS], U32, name="kw", tag="k_bytes_then_kw", align_bytes=64)
+        for h in range(2):
+            cols = slice(h * HALF, (h + 1) * HALF)
+            nc.vector.tensor_copy(kw[:, cols], k_words[:].indirect(offsets[:, h * HALF // 16 : (h + 1) * HALF // 16]))
+            a = ps.tile([P, HALF], F32, name="a%d" % h)
+            nc.tensor.matmul_mx(out=a[:], lhsT=q_codes[:].bitcast(FP8X4), lhsT_scale=q_scales[:], rhs=kw[:, cols].bitcast(FP8X4), rhs_scale=ks[:, cols], start=True, stop=True)
+            nc.scalar.activation(e0[:, cols], a[:], ACT.Exp)
+            scores.append(a)
+        for h in range(2):
+            nc.scalar.activation(s0[:, h * HALF : (h + 1) * HALF], scores[h][:], ACT.Sigmoid)
+        s0_sq = sb.tile([P, SLOTS], F32, name="s0_sq")
+        nc.scalar.activation(s0_sq[:], s0[:], ACT.Square)
+
+        result = sb.tile([P, T], F32, name="result", tag="keys_then_old")
+        nc.sync.dma_start(result[:], old)
+
+        vs = sb.tile([P, SLOTS], U8, name="vs", align_bytes=64)
+        nc.vector.tensor_copy(vs[:], v_bytes[:].indirect(offsets[:]))
+        g_codes = sb.tile([P, Q], U32, name="g_codes", align_bytes=64)
+        g_scales = sb.tile([P, Q], U8, name="g_scales", align_bytes=64)
+        nc.vector.quantize_mx(out=g_codes[:].bitcast(FP8X4), scales=g_scales[:], in_=g_bf[:].rearrange("p q j -> p (q j)"))
+        vw = sb.tile([P, SLOTS], U32, name="vw", tag="v_bytes_then_vw", align_bytes=64)
+        nc.vector.tensor_copy(vw[:], v_words[:].indirect(offsets[:]))
+        c0 = ps.tile([P, SLOTS], F32, name="c0")
+        nc.tensor.matmul_mx(out=c0[:], lhsT=g_codes[:].bitcast(FP8X4), lhsT_scale=g_scales[:], rhs=vw[:].bitcast(FP8X4), rhs_scale=vs[:], start=True, stop=True)
+
+        part_exp = sb.tile([P, SLOTS], F32, name="part_exp", tag="v_words_then_part_exp")
+        nc.vector.tensor_scalar(part_exp[:], e0[:], mix_exp[:], None, ALU.mult)
+        part = sb.tile([P, SLOTS], F32, name="part")
+        z = sb.tile([P, 1], F32, name="z")
+        nc.vector.scalar_tensor_tensor(part[:], s0[:], mix_sig[:], part_exp[:], ALU.mult, ALU.add, accum_out=z[:])
+        rz = sb.tile([P, 1], F32, name="rz")
+        nc.vector.reciprocal(rz[:], z[:])
+        slope = sb.tile([P, SLOTS], F32, name="slope")
+        nc.vector.scalar_tensor_tensor(slope[:], s0_sq[:], mix_sig_neg[:], part[:], ALU.mult, ALU.add)
+        rz512 = sb.tile([P, 1], F32, name="rz512")
+        nc.scalar.activation(rz512[:], rz[:], ACT.Copy, scale=512.0)
+        weighted = sb.tile([P, SLOTS], F32, name="weighted")
+        mean = sb.tile([P, 1], F32, name="mean")
+        nc.vector.scalar_tensor_tensor(weighted[:], c0[:], rz[:], part[:], ALU.mult, ALU.mult, accum_out=mean[:])
+        dp512 = sb.tile([P, SLOTS], F32, name="dp512")
+        nc.vector.tensor_scalar(dp512[:], c0[:], mean[:], rz512[:], ALU.subtract, ALU.mult)
+        nc.vector.tensor_tensor(placed[:].indirect(offsets[:]), dp512[:], slope[:], ALU.mult)
+
+        for c in range(T // OUT_CHUNK):
+            cols = slice(c * OUT_CHUNK, (c + 1) * OUT_CHUNK)
+            nc.vector.tensor_tensor(result[:, cols], result[:, cols], placed[:, cols], ALU.add)
+            nc.sync.dma_start(out[:, cols], result[:, cols])

@@ -18,7 +18,7 @@ ACT = mybir.ActivationFunctionType
 P = 128
 PACK = 4
 HALF = SLOTS // 2
-OUT_CHUNK = 512
+OUT_EDGES = [0, 256, 768, 1280, 1792, 2048]
 
 
 def tile_attend_bmixedparts_s_kernel(tc, query, keys_words, keys_scales, share, gout, vals_words, vals_scales, old, offs, out):
@@ -32,25 +32,27 @@ def tile_attend_bmixedparts_s_kernel(tc, query, keys_words, keys_scales, share, 
 
         k_bytes = sb.tile([P, T], U8, name="k_bytes", tag="k_bytes_then_kw", align_bytes=64)
         v_bytes = sb.tile([P, T], U8, name="v_bytes", tag="v_bytes_then_vw", align_bytes=64)
-        nc.vector.memset(k_bytes[:].bitcast(I32), 0)
+        nc.vector.memset(k_bytes[:, : T // 2].bitcast(I32), 0)
+        nc.gpsimd.memset(k_bytes[:, T // 2 :].bitcast(I32), 0)
         nc.vector.memset(v_bytes[:].bitcast(I32), 0)
 
-        q_raw = sb.tile([P, PACK, Q], F32, name="q_raw", tag="raw")
-        nc.scalar.dma_start(q_raw[:], query.rearrange("(p j) q -> p j q", j=PACK))
+        q_raw = sb.tile([P, PACK, Q], F32, name="q_raw")
+        nc.sync.dma_start(q_raw[:], query.rearrange("(p j) q -> p j q", j=PACK))
+        mix_exp = sb.tile([P, 1], F32, name="mix_exp")
+        nc.sync.dma_start(mix_exp[:], share)
+        for quad in range(4):
+            nc.sync.dma_start(k_bytes[32 * quad : 32 * quad + 4, :].bitcast(I32), keys_scales[0, 4 * quad : 4 * quad + 4, :].bitcast(I32))
         k_words = sb.tile([P, T], U32, name="k_words", tag="keys_then_old")
         nc.sync.dma_start(k_words[:].bitcast(I32), keys_words[0].rearrange("p t r -> p (t r)").bitcast(I32))
+        g_raw = sb.tile([P, PACK, Q], F32, name="g_raw")
+        nc.sync.dma_start(g_raw[:], gout.rearrange("(p j) q -> p j q", j=PACK))
         for quad in range(4):
-            nc.scalar.dma_start(k_bytes[32 * quad : 32 * quad + 4, :].bitcast(I32), keys_scales[0, 4 * quad : 4 * quad + 4, :].bitcast(I32))
-        mix_exp = sb.tile([P, 1], F32, name="mix_exp")
-        nc.gpsimd.dma_start(mix_exp[:], share)
+            nc.sync.dma_start(v_bytes[32 * quad : 32 * quad + 4, :].bitcast(I32), vals_scales[0, 4 * quad : 4 * quad + 4, :].bitcast(I32))
         v_words = sb.tile([P, T], U32, name="v_words", tag="v_words_then_part_exp")
         nc.sync.dma_start(v_words[:].bitcast(I32), vals_words[0].rearrange("p t r -> p (t r)").bitcast(I32))
-        for quad in range(4):
-            nc.gpsimd.dma_start(v_bytes[32 * quad : 32 * quad + 4, :].bitcast(I32), vals_scales[0, 4 * quad : 4 * quad + 4, :].bitcast(I32))
 
         placed = sb.tile([P, T], F32, name="placed")
-        nc.vector.memset(placed[:, : T // 2 - 1], 0.0)
-        nc.vector.memset(placed[:, T // 2 - 1 :], 0.0)
+        nc.vector.memset(placed[:], 0.0)
 
         mix_sig = sb.tile([P, 1], F32, name="mix_sig")
         mix_sig_neg = sb.tile([P, 1], F32, name="mix_sig_neg")
@@ -58,20 +60,20 @@ def tile_attend_bmixedparts_s_kernel(tc, query, keys_words, keys_scales, share, 
         nc.scalar.activation(mix_sig_neg[:], mix_exp[:], ACT.Copy, bias=-3.0, scale=3.0)
 
         q_bf = sb.tile([P, Q, PACK], BF16, name="q_bf", align_bytes=64)
-        nc.vector.tensor_copy(q_bf[:], q_raw[:].rearrange("p j q -> p q j"))
+        nc.scalar.copy(q_bf[:], q_raw[:].rearrange("p j q -> p q j"))
         ks = sb.tile([P, SLOTS], U8, name="ks", align_bytes=64)
         nc.vector.tensor_copy(ks[:], k_bytes[:].indirect(offsets[:]))
         q_codes = sb.tile([P, Q], U32, name="q_codes", align_bytes=64)
         q_scales = sb.tile([P, Q], U8, name="q_scales", align_bytes=64)
         nc.vector.quantize_mx(out=q_codes[:].bitcast(FP8X4), scales=q_scales[:], in_=q_bf[:].rearrange("p q j -> p (q j)"))
 
-        g_raw = sb.tile([P, PACK, Q], F32, name="g_raw", tag="raw")
-        nc.scalar.dma_start(g_raw[:], gout.rearrange("(p j) q -> p j q", j=PACK))
         g_bf = sb.tile([P, Q, PACK], BF16, name="g_bf", align_bytes=64)
         nc.scalar.copy(g_bf[:], g_raw[:].rearrange("p j q -> p q j"))
 
         e0 = sb.tile([P, SLOTS], F32, name="e0")
         s0 = sb.tile([P, SLOTS], F32, name="s0")
+        e0_sums = sb.tile([P, 2], F32, name="e0_sums")
+        s0_sums = sb.tile([P, 2], F32, name="s0_sums")
         scores = []
         kw = sb.tile([P, SLOTS], U32, name="kw", tag="k_bytes_then_kw", align_bytes=64)
         for h in range(2):
@@ -79,12 +81,13 @@ def tile_attend_bmixedparts_s_kernel(tc, query, keys_words, keys_scales, share, 
             nc.vector.tensor_copy(kw[:, cols], k_words[:].indirect(offsets[:, h * HALF // 16 : (h + 1) * HALF // 16]))
             a = ps.tile([P, HALF], F32, name="a%d" % h)
             nc.tensor.matmul_mx(out=a[:], lhsT=q_codes[:].bitcast(FP8X4), lhsT_scale=q_scales[:], rhs=kw[:, cols].bitcast(FP8X4), rhs_scale=ks[:, cols], start=True, stop=True)
-            nc.scalar.activation(e0[:, cols], a[:], ACT.Exp)
+            nc.scalar.activation(e0[:, cols], a[:], ACT.Exp, accum_out=e0_sums[:, h : h + 1])
             scores.append(a)
         for h in range(2):
-            nc.scalar.activation(s0[:, h * HALF : (h + 1) * HALF], scores[h][:], ACT.Sigmoid)
+            nc.scalar.activation(s0[:, h * HALF : (h + 1) * HALF], scores[h][:], ACT.Sigmoid, accum_out=s0_sums[:, h : h + 1])
         s0_sq = sb.tile([P, SLOTS], F32, name="s0_sq")
-        nc.scalar.activation(s0_sq[:], s0[:], ACT.Square)
+        for h in range(2):
+            nc.scalar.activation(s0_sq[:, h * HALF : (h + 1) * HALF], s0[:, h * HALF : (h + 1) * HALF], ACT.Square)
 
         result = sb.tile([P, T], F32, name="result", tag="keys_then_old")
         nc.sync.dma_start(result[:], old)
@@ -99,25 +102,34 @@ def tile_attend_bmixedparts_s_kernel(tc, query, keys_words, keys_scales, share, 
         c0 = ps.tile([P, SLOTS], F32, name="c0")
         nc.tensor.matmul_mx(out=c0[:], lhsT=g_codes[:].bitcast(FP8X4), lhsT_scale=g_scales[:], rhs=vw[:].bitcast(FP8X4), rhs_scale=vs[:], start=True, stop=True)
 
-        part_exp = sb.tile([P, SLOTS], F32, name="part_exp", tag="v_words_then_part_exp")
-        nc.vector.tensor_scalar(part_exp[:], e0[:], mix_exp[:], None, ALU.mult)
+        exp_terms = sb.tile([P, SLOTS + 1], F32, name="exp_terms", tag="v_words_then_part_exp")
+        part_exp, z_exp = exp_terms[:, :SLOTS], exp_terms[:, SLOTS:]
+        nc.vector.tensor_scalar(z_exp, e0_sums[:, 0:1], e0_sums[:, 1:2], mix_exp[:], ALU.add, ALU.mult)
+        nc.vector.tensor_scalar(part_exp, e0[:], mix_exp[:], None, ALU.mult)
+
+        lo_half, hi_half = slice(0, HALF), slice(HALF, SLOTS)
         part = sb.tile([P, SLOTS], F32, name="part")
-        z = sb.tile([P, 1], F32, name="z")
-        nc.vector.scalar_tensor_tensor(part[:], s0[:], mix_sig[:], part_exp[:], ALU.mult, ALU.add, accum_out=z[:])
-        rz = sb.tile([P, 1], F32, name="rz")
-        nc.vector.reciprocal(rz[:], z[:])
         slope = sb.tile([P, SLOTS], F32, name="slope")
-        nc.vector.scalar_tensor_tensor(slope[:], s0_sq[:], mix_sig_neg[:], part[:], ALU.mult, ALU.add)
+        z_lo = sb.tile([P, 1], F32, name="z_lo")
+        z = sb.tile([P, 1], F32, name="z")
+        rz = sb.tile([P, 1], F32, name="rz")
+        nc.vector.scalar_tensor_tensor(part[:, lo_half], s0[:, lo_half], mix_sig[:], part_exp[:, lo_half], ALU.mult, ALU.add)
+        nc.vector.tensor_scalar(z_lo[:], s0_sums[:, 0:1], mix_sig[:], z_exp, ALU.mult, ALU.add)
+        nc.vector.scalar_tensor_tensor(part[:, hi_half], s0[:, hi_half], mix_sig[:], part_exp[:, hi_half], ALU.mult, ALU.add)
+        nc.vector.tensor_scalar(z[:], s0_sums[:, 1:2], mix_sig[:], z_lo[:], ALU.mult, ALU.add)
+        nc.vector.scalar_tensor_tensor(slope[:, lo_half], s0_sq[:, lo_half], mix_sig_neg[:], part[:, lo_half], ALU.mult, ALU.add)
+        nc.vector.reciprocal(rz[:], z[:])
         rz512 = sb.tile([P, 1], F32, name="rz512")
         nc.scalar.activation(rz512[:], rz[:], ACT.Copy, scale=512.0)
         weighted = sb.tile([P, SLOTS], F32, name="weighted")
         mean = sb.tile([P, 1], F32, name="mean")
         nc.vector.scalar_tensor_tensor(weighted[:], c0[:], rz[:], part[:], ALU.mult, ALU.mult, accum_out=mean[:])
+        nc.vector.scalar_tensor_tensor(slope[:, hi_half], s0_sq[:, hi_half], mix_sig_neg[:], part[:, hi_half], ALU.mult, ALU.add)
         dp512 = sb.tile([P, SLOTS], F32, name="dp512")
         nc.vector.tensor_scalar(dp512[:], c0[:], mean[:], rz512[:], ALU.subtract, ALU.mult)
         nc.vector.tensor_tensor(placed[:].indirect(offsets[:]), dp512[:], slope[:], ALU.mult)
 
-        for c in range(T // OUT_CHUNK):
-            cols = slice(c * OUT_CHUNK, (c + 1) * OUT_CHUNK)
+        for lo, hi in zip(OUT_EDGES[:-1], OUT_EDGES[1:]):
+            cols = slice(lo, hi)
             nc.vector.tensor_tensor(result[:, cols], result[:, cols], placed[:, cols], ALU.add)
             nc.sync.dma_start(out[:, cols], result[:, cols])

@@ -18,6 +18,8 @@ ACT = mybir.ActivationFunctionType
 P = 128
 PACK = 4
 HALF = SLOTS // 2
+KEYS_FIRST = 512
+KEY_PIECES = [(0, 256), (256, 384), (384, 512)]
 OUT_EDGES = [0, 256, 768, 1280, 1792, 2048]
 
 
@@ -32,22 +34,23 @@ def tile_attend_bmixedparts_s_kernel(tc, query, keys_words, keys_scales, share, 
 
         k_bytes = sb.tile([P, T], U8, name="k_bytes", tag="k_bytes_then_kw", align_bytes=64)
         v_bytes = sb.tile([P, T], U8, name="v_bytes", tag="v_bytes_then_vw", align_bytes=64)
-        nc.vector.memset(k_bytes[:, : T // 2].bitcast(I32), 0)
-        nc.gpsimd.memset(k_bytes[:, T // 2 :].bitcast(I32), 0)
+        nc.vector.memset(k_bytes[:].bitcast(I32), 0)
         nc.vector.memset(v_bytes[:].bitcast(I32), 0)
 
         q_raw = sb.tile([P, PACK, Q], F32, name="q_raw")
         nc.sync.dma_start(q_raw[:], query.rearrange("(p j) q -> p j q", j=PACK))
-        mix_exp = sb.tile([P, 1], F32, name="mix_exp")
-        nc.sync.dma_start(mix_exp[:], share)
-        for quad in range(4):
-            nc.sync.dma_start(k_bytes[32 * quad : 32 * quad + 4, :].bitcast(I32), keys_scales[0, 4 * quad : 4 * quad + 4, :].bitcast(I32))
         k_words = sb.tile([P, T], U32, name="k_words", tag="keys_then_old")
-        nc.sync.dma_start(k_words[:].bitcast(I32), keys_words[0].rearrange("p t r -> p (t r)").bitcast(I32))
+        keys_i32 = keys_words[0].rearrange("p t r -> p (t r)").bitcast(I32)
+        nc.sync.dma_start(k_words[:, :KEYS_FIRST].bitcast(I32), keys_i32[:, :KEYS_FIRST])
+        for r in range(4):
+            nc.sync.dma_start(k_bytes[r:P:32, :].bitcast(I32), keys_scales[0, r:16:4, :].bitcast(I32))
+        nc.sync.dma_start(k_words[:, KEYS_FIRST:].bitcast(I32), keys_i32[:, KEYS_FIRST:])
         g_raw = sb.tile([P, PACK, Q], F32, name="g_raw")
         nc.sync.dma_start(g_raw[:], gout.rearrange("(p j) q -> p j q", j=PACK))
-        for quad in range(4):
-            nc.sync.dma_start(v_bytes[32 * quad : 32 * quad + 4, :].bitcast(I32), vals_scales[0, 4 * quad : 4 * quad + 4, :].bitcast(I32))
+        mix_exp = sb.tile([P, 1], F32, name="mix_exp")
+        nc.sync.dma_start(mix_exp[:], share)
+        for r in range(4):
+            nc.sync.dma_start(v_bytes[r:P:32, :].bitcast(I32), vals_scales[0, r:16:4, :].bitcast(I32))
         v_words = sb.tile([P, T], U32, name="v_words", tag="v_words_then_part_exp")
         nc.sync.dma_start(v_words[:].bitcast(I32), vals_words[0].rearrange("p t r -> p (t r)").bitcast(I32))
 
@@ -72,19 +75,18 @@ def tile_attend_bmixedparts_s_kernel(tc, query, keys_words, keys_scales, share, 
 
         e0 = sb.tile([P, SLOTS], F32, name="e0")
         s0 = sb.tile([P, SLOTS], F32, name="s0")
-        e0_sums = sb.tile([P, 2], F32, name="e0_sums")
-        s0_sums = sb.tile([P, 2], F32, name="s0_sums")
-        scores = []
+        e0_sums = sb.tile([P, len(KEY_PIECES)], F32, name="e0_sums")
+        s0_sums = sb.tile([P, len(KEY_PIECES)], F32, name="s0_sums")
         kw = sb.tile([P, SLOTS], U32, name="kw", tag="k_bytes_then_kw", align_bytes=64)
-        for h in range(2):
-            cols = slice(h * HALF, (h + 1) * HALF)
-            nc.vector.tensor_copy(kw[:, cols], k_words[:].indirect(offsets[:, h * HALF // 16 : (h + 1) * HALF // 16]))
-            a = ps.tile([P, HALF], F32, name="a%d" % h)
-            nc.tensor.matmul_mx(out=a[:], lhsT=q_codes[:].bitcast(FP8X4), lhsT_scale=q_scales[:], rhs=kw[:, cols].bitcast(FP8X4), rhs_scale=ks[:, cols], start=True, stop=True)
-            nc.scalar.activation(e0[:, cols], a[:], ACT.Exp, accum_out=e0_sums[:, h : h + 1])
+        scores = []
+        for n, (lo, hi) in enumerate(KEY_PIECES):
+            nc.vector.tensor_copy(kw[:, lo:hi], k_words[:].indirect(offsets[:, lo // 16 : hi // 16]))
+            a = ps.tile([P, hi - lo], F32, name="a%d" % n)
+            nc.tensor.matmul_mx(out=a[:], lhsT=q_codes[:].bitcast(FP8X4), lhsT_scale=q_scales[:], rhs=kw[:, lo:hi].bitcast(FP8X4), rhs_scale=ks[:, lo:hi], start=True, stop=True)
+            nc.scalar.activation(e0[:, lo:hi], a[:], ACT.Exp, accum_out=e0_sums[:, n : n + 1])
             scores.append(a)
-        for h in range(2):
-            nc.scalar.activation(s0[:, h * HALF : (h + 1) * HALF], scores[h][:], ACT.Sigmoid, accum_out=s0_sums[:, h : h + 1])
+        for n, (lo, hi) in enumerate(KEY_PIECES):
+            nc.scalar.activation(s0[:, lo:hi], scores[n][:], ACT.Sigmoid, accum_out=s0_sums[:, n : n + 1])
         s0_sq = sb.tile([P, SLOTS], F32, name="s0_sq")
         for h in range(2):
             nc.scalar.activation(s0_sq[:, h * HALF : (h + 1) * HALF], s0[:, h * HALF : (h + 1) * HALF], ACT.Square)
@@ -104,19 +106,19 @@ def tile_attend_bmixedparts_s_kernel(tc, query, keys_words, keys_scales, share, 
 
         exp_terms = sb.tile([P, SLOTS + 1], F32, name="exp_terms", tag="v_words_then_part_exp")
         part_exp, z_exp = exp_terms[:, :SLOTS], exp_terms[:, SLOTS:]
-        nc.vector.tensor_scalar(z_exp, e0_sums[:, 0:1], e0_sums[:, 1:2], mix_exp[:], ALU.add, ALU.mult)
+        exp_sums = sb.tile([P, len(KEY_PIECES)], F32, name="exp_sums")
+        nc.vector.tensor_scalar(exp_sums[:], e0_sums[:], mix_exp[:], None, ALU.mult, ALU.add, accum_out=z_exp)
         nc.vector.tensor_scalar(part_exp, e0[:], mix_exp[:], None, ALU.mult)
 
         lo_half, hi_half = slice(0, HALF), slice(HALF, SLOTS)
         part = sb.tile([P, SLOTS], F32, name="part")
         slope = sb.tile([P, SLOTS], F32, name="slope")
-        z_lo = sb.tile([P, 1], F32, name="z_lo")
+        sig_sums = sb.tile([P, len(KEY_PIECES)], F32, name="sig_sums")
         z = sb.tile([P, 1], F32, name="z")
         rz = sb.tile([P, 1], F32, name="rz")
         nc.vector.scalar_tensor_tensor(part[:, lo_half], s0[:, lo_half], mix_sig[:], part_exp[:, lo_half], ALU.mult, ALU.add)
-        nc.vector.tensor_scalar(z_lo[:], s0_sums[:, 0:1], mix_sig[:], z_exp, ALU.mult, ALU.add)
         nc.vector.scalar_tensor_tensor(part[:, hi_half], s0[:, hi_half], mix_sig[:], part_exp[:, hi_half], ALU.mult, ALU.add)
-        nc.vector.tensor_scalar(z[:], s0_sums[:, 1:2], mix_sig[:], z_lo[:], ALU.mult, ALU.add)
+        nc.vector.tensor_scalar(sig_sums[:], s0_sums[:], mix_sig[:], z_exp, ALU.mult, ALU.add, accum_out=z[:])
         nc.vector.scalar_tensor_tensor(slope[:, lo_half], s0_sq[:, lo_half], mix_sig_neg[:], part[:, lo_half], ALU.mult, ALU.add)
         nc.vector.reciprocal(rz[:], z[:])
         rz512 = sb.tile([P, 1], F32, name="rz512")

@@ -19,6 +19,7 @@ P = 128
 PACK = 4
 HALF = SLOTS // 2
 KEYS_FIRST = 512
+V_PLANE = 4
 KEY_PIECES = [(0, 256), (256, 384), (384, 512)]
 OUT_EDGES = [0, 256, 768, 1280, 1792, 2048]
 
@@ -50,7 +51,7 @@ def tile_attend_bmixedparts_s_kernel(tc, query, keys_words, keys_scales, share, 
         mix_exp = sb.tile([P, 1], F32, name="mix_exp")
         nc.sync.dma_start(mix_exp[:], share)
         for r in range(4):
-            nc.sync.dma_start(v_bytes[r:P:32, :].bitcast(I32), vals_scales[0, r:16:4, :].bitcast(I32))
+            nc.sync.dma_start(v_bytes[V_PLANE + r : P : 32, :].bitcast(I32), vals_scales[0, r:16:4, :].bitcast(I32))
         v_words = sb.tile([P, T], U32, name="v_words", tag="v_words_then_part_exp")
         nc.sync.dma_start(v_words[:].bitcast(I32), vals_words[0].rearrange("p t r -> p (t r)").bitcast(I32))
 
@@ -102,7 +103,7 @@ def tile_attend_bmixedparts_s_kernel(tc, query, keys_words, keys_scales, share, 
         vw = sb.tile([P, SLOTS], U32, name="vw", tag="v_bytes_then_vw", align_bytes=64)
         nc.vector.tensor_copy(vw[:], v_words[:].indirect(offsets[:]))
         c0 = ps.tile([P, SLOTS], F32, name="c0")
-        nc.tensor.matmul_mx(out=c0[:], lhsT=g_codes[:].bitcast(FP8X4), lhsT_scale=g_scales[:], rhs=vw[:].bitcast(FP8X4), rhs_scale=vs[:], start=True, stop=True)
+        nc.tensor.matmul_mx(out=c0[:], lhsT=g_codes[:].bitcast(FP8X4), lhsT_scale=g_scales[:], rhs=vw[:].bitcast(FP8X4), rhs_scale=vs[V_PLANE:, :], start=True, stop=True)
 
         exp_terms = sb.tile([P, SLOTS + 1], F32, name="exp_terms", tag="v_words_then_part_exp")
         part_exp, z_exp = exp_terms[:, :SLOTS], exp_terms[:, SLOTS:]

@@ -31,10 +31,9 @@ def tile_attend_bmixedparts_s_kernel(tc, query, keys_words, keys_scales, share, 
         ps = ctx.enter_context(tc.psum_pool(name="ps", bufs=1))
 
         offsets = sb.tile([P, SLOTS // 16], U16, name="offsets")
-        nc.sync.dma_start(offsets[:], offs)
 
         k_bytes = sb.tile([P, T], U8, name="k_bytes", tag="k_bytes_then_kw", align_bytes=64)
-        v_bytes = sb.tile([P, T], U8, name="v_bytes", tag="v_bytes_then_vw", align_bytes=64)
+        v_bytes = sb.tile([P, T], U8, name="v_bytes", tag="v_bytes_then_part_exp_lo", align_bytes=64)
         nc.vector.memset(k_bytes[:].bitcast(I32), 0)
         nc.vector.memset(v_bytes[:].bitcast(I32), 0)
 
@@ -43,6 +42,7 @@ def tile_attend_bmixedparts_s_kernel(tc, query, keys_words, keys_scales, share, 
         k_words = sb.tile([P, T], U32, name="k_words", tag="keys_then_old")
         keys_i32 = keys_words[0].rearrange("p t r -> p (t r)").bitcast(I32)
         nc.sync.dma_start(k_words[:, :KEYS_FIRST].bitcast(I32), keys_i32[:, :KEYS_FIRST])
+        nc.sync.dma_start(offsets[:], offs)
         for r in range(4):
             nc.sync.dma_start(k_bytes[r:P:32, :].bitcast(I32), keys_scales[0, r:16:4, :].bitcast(I32))
         nc.sync.dma_start(k_words[:, KEYS_FIRST:].bitcast(I32), keys_i32[:, KEYS_FIRST:])
@@ -58,9 +58,12 @@ def tile_attend_bmixedparts_s_kernel(tc, query, keys_words, keys_scales, share, 
         placed = sb.tile([P, T], F32, name="placed")
         nc.vector.memset(placed[:], 0.0)
 
-        mix_sig = sb.tile([P, 1], F32, name="mix_sig")
+        pieces = len(KEY_PIECES)
+        mixes = sb.tile([P, 2 * pieces], F32, name="mixes")
+        mix_sig = mixes[:, pieces : pieces + 1]
         mix_sig_neg = sb.tile([P, 1], F32, name="mix_sig_neg")
-        nc.scalar.activation(mix_sig[:], mix_exp[:], ACT.Copy, bias=3.0, scale=-3.0)
+        nc.scalar.activation(mixes[:, :pieces], mix_exp[:].to_broadcast([P, pieces]), ACT.Copy)
+        nc.scalar.activation(mixes[:, pieces:], mix_exp[:].to_broadcast([P, pieces]), ACT.Copy, bias=3.0, scale=-3.0)
         nc.scalar.activation(mix_sig_neg[:], mix_exp[:], ACT.Copy, bias=-3.0, scale=3.0)
 
         q_bf = sb.tile([P, Q, PACK], BF16, name="q_bf", align_bytes=64)
@@ -74,20 +77,21 @@ def tile_attend_bmixedparts_s_kernel(tc, query, keys_words, keys_scales, share, 
         g_bf = sb.tile([P, Q, PACK], BF16, name="g_bf", align_bytes=64)
         nc.scalar.copy(g_bf[:], g_raw[:].rearrange("p j q -> p q j"))
 
-        e0 = sb.tile([P, SLOTS], F32, name="e0")
+        e0_lo = sb.tile([P, HALF], F32, name="e0_lo", tag="e0_lo_then_vw", align_bytes=64)
+        e0_hi = sb.tile([P, HALF], F32, name="e0_hi")
         s0 = sb.tile([P, SLOTS], F32, name="s0")
-        e0_sums = sb.tile([P, len(KEY_PIECES)], F32, name="e0_sums")
-        s0_sums = sb.tile([P, len(KEY_PIECES)], F32, name="s0_sums")
+        sums = sb.tile([P, 2 * pieces], F32, name="sums")
         kw = sb.tile([P, SLOTS], U32, name="kw", tag="k_bytes_then_kw", align_bytes=64)
         scores = []
         for n, (lo, hi) in enumerate(KEY_PIECES):
             nc.vector.tensor_copy(kw[:, lo:hi], k_words[:].indirect(offsets[:, lo // 16 : hi // 16]))
             a = ps.tile([P, hi - lo], F32, name="a%d" % n)
             nc.tensor.matmul_mx(out=a[:], lhsT=q_codes[:].bitcast(FP8X4), lhsT_scale=q_scales[:], rhs=kw[:, lo:hi].bitcast(FP8X4), rhs_scale=ks[:, lo:hi], start=True, stop=True)
-            nc.scalar.activation(e0[:, lo:hi], a[:], ACT.Exp, accum_out=e0_sums[:, n : n + 1])
+            e0_piece = e0_lo[:, lo:hi] if hi <= HALF else e0_hi[:, lo - HALF : hi - HALF]
+            nc.scalar.activation(e0_piece, a[:], ACT.Exp, accum_out=sums[:, n : n + 1])
             scores.append(a)
         for n, (lo, hi) in enumerate(KEY_PIECES):
-            nc.scalar.activation(s0[:, lo:hi], scores[n][:], ACT.Sigmoid, accum_out=s0_sums[:, n : n + 1])
+            nc.scalar.activation(s0[:, lo:hi], scores[n][:], ACT.Sigmoid, accum_out=sums[:, pieces + n : pieces + n + 1])
         s0_sq = sb.tile([P, SLOTS], F32, name="s0_sq")
         for h in range(2):
             nc.scalar.activation(s0_sq[:, h * HALF : (h + 1) * HALF], s0[:, h * HALF : (h + 1) * HALF], ACT.Square)
@@ -100,33 +104,31 @@ def tile_attend_bmixedparts_s_kernel(tc, query, keys_words, keys_scales, share, 
         g_codes = sb.tile([P, Q], U32, name="g_codes", align_bytes=64)
         g_scales = sb.tile([P, Q], U8, name="g_scales", align_bytes=64)
         nc.vector.quantize_mx(out=g_codes[:].bitcast(FP8X4), scales=g_scales[:], in_=g_bf[:].rearrange("p q j -> p (q j)"))
-        vw = sb.tile([P, SLOTS], U32, name="vw", tag="v_bytes_then_vw", align_bytes=64)
+        part_exp_lo = sb.tile([P, HALF], F32, name="part_exp_lo", tag="v_bytes_then_part_exp_lo", align_bytes=64)
+        nc.vector.tensor_scalar(part_exp_lo[:], e0_lo[:], mix_exp[:], None, ALU.mult)
+        vw = sb.tile([P, SLOTS], U32, name="vw", tag="e0_lo_then_vw", align_bytes=64)
         nc.vector.tensor_copy(vw[:], v_words[:].indirect(offsets[:]))
         c0 = ps.tile([P, SLOTS], F32, name="c0")
         nc.tensor.matmul_mx(out=c0[:], lhsT=g_codes[:].bitcast(FP8X4), lhsT_scale=g_scales[:], rhs=vw[:].bitcast(FP8X4), rhs_scale=vs[V_PLANE:, :], start=True, stop=True)
 
-        exp_terms = sb.tile([P, SLOTS + 1], F32, name="exp_terms", tag="v_words_then_part_exp")
-        part_exp, z_exp = exp_terms[:, :SLOTS], exp_terms[:, SLOTS:]
-        exp_sums = sb.tile([P, len(KEY_PIECES)], F32, name="exp_sums")
-        nc.vector.tensor_scalar(exp_sums[:], e0_sums[:], mix_exp[:], None, ALU.mult, ALU.add, accum_out=z_exp)
-        nc.vector.tensor_scalar(part_exp, e0[:], mix_exp[:], None, ALU.mult)
-
         lo_half, hi_half = slice(0, HALF), slice(HALF, SLOTS)
-        part = sb.tile([P, SLOTS], F32, name="part")
+        late = sb.tile([P, SLOTS + HALF + 2 * pieces], F32, name="late", tag="v_words_then_part_exp")
+        part, part_exp_hi, mixed_sums = late[:, :SLOTS], late[:, SLOTS : SLOTS + HALF], late[:, SLOTS + HALF :]
+        nc.vector.tensor_scalar(part_exp_hi, e0_hi[:], mix_exp[:], None, ALU.mult)
+
         slope = sb.tile([P, SLOTS], F32, name="slope")
-        sig_sums = sb.tile([P, len(KEY_PIECES)], F32, name="sig_sums")
         z = sb.tile([P, 1], F32, name="z")
         rz = sb.tile([P, 1], F32, name="rz")
-        nc.vector.scalar_tensor_tensor(part[:, lo_half], s0[:, lo_half], mix_sig[:], part_exp[:, lo_half], ALU.mult, ALU.add)
-        nc.vector.scalar_tensor_tensor(part[:, hi_half], s0[:, hi_half], mix_sig[:], part_exp[:, hi_half], ALU.mult, ALU.add)
-        nc.vector.tensor_scalar(sig_sums[:], s0_sums[:], mix_sig[:], z_exp, ALU.mult, ALU.add, accum_out=z[:])
-        nc.vector.scalar_tensor_tensor(slope[:, lo_half], s0_sq[:, lo_half], mix_sig_neg[:], part[:, lo_half], ALU.mult, ALU.add)
+        nc.vector.scalar_tensor_tensor(part[:, lo_half], s0[:, lo_half], mix_sig, part_exp_lo[:], ALU.mult, ALU.add)
+        nc.vector.scalar_tensor_tensor(mixed_sums, sums[:], 1.0, mixes[:], ALU.mult, ALU.mult, accum_out=z[:])
+        nc.vector.scalar_tensor_tensor(part[:, hi_half], s0[:, hi_half], mix_sig, part_exp_hi, ALU.mult, ALU.add)
         nc.vector.reciprocal(rz[:], z[:])
+        nc.vector.scalar_tensor_tensor(slope[:, lo_half], s0_sq[:, lo_half], mix_sig_neg[:], part[:, lo_half], ALU.mult, ALU.add)
         rz512 = sb.tile([P, 1], F32, name="rz512")
         nc.scalar.activation(rz512[:], rz[:], ACT.Copy, scale=512.0)
         weighted = sb.tile([P, SLOTS], F32, name="weighted")
         mean = sb.tile([P, 1], F32, name="mean")
-        nc.vector.scalar_tensor_tensor(weighted[:], c0[:], rz[:], part[:], ALU.mult, ALU.mult, accum_out=mean[:])
+        nc.vector.scalar_tensor_tensor(weighted[:], c0[:], rz[:], part, ALU.mult, ALU.mult, accum_out=mean[:])
         nc.vector.scalar_tensor_tensor(slope[:, hi_half], s0_sq[:, hi_half], mix_sig_neg[:], part[:, hi_half], ALU.mult, ALU.add)
         dp512 = sb.tile([P, SLOTS], F32, name="dp512")
         nc.vector.tensor_scalar(dp512[:], c0[:], mean[:], rz512[:], ALU.subtract, ALU.mult)

from contextlib import ExitStack

import concourse.mybir as mybir

D, E, T, SLOTS, Q = 512, 512, 2048, 512, 128
FLOPS = 2 * Q * SLOTS * (D + E)

F32 = mybir.dt.float32
BF16 = mybir.dt.bfloat16
I32 = mybir.dt.int32
U32 = mybir.dt.uint32
U16 = mybir.dt.uint16
U8 = mybir.dt.uint8
FP8X4 = mybir.dt.float8_e4m3fn_x4
ALU = mybir.AluOpType
ACT = mybir.ActivationFunctionType

P = 128
PACK = 4
HALF = SLOTS // 2
KEYS_FIRST = 512
V_PLANE = 4
KEY_PIECES = [(0, 256), (256, 384), (384, 512)]
OUT_EDGES = [0, 256, 768, 1280, 1792, 2048]


def tile_attend_bmixedparts_s_kernel(tc, query, keys_words, keys_scales, share, gout, vals_words, vals_scales, old, offs, out):
    nc = tc.nc
    with ExitStack() as ctx:
        sb = ctx.enter_context(tc.tile_pool(name="sb", bufs=1))
        ps = ctx.enter_context(tc.psum_pool(name="ps", bufs=1))

        offsets = sb.tile([P, SLOTS // 16], U16, name="offsets")

        k_bytes = sb.tile([P, T], U8, name="k_bytes", tag="k_bytes_then_kw", align_bytes=64)
        v_bytes = sb.tile([P, T], U8, name="v_bytes", tag="v_bytes_then_part_exp_lo", align_bytes=64)
        nc.vector.memset(k_bytes[:].bitcast(I32), 0)
        nc.vector.memset(v_bytes[:].bitcast(I32), 0)

        q_raw = sb.tile([P, PACK, Q], F32, name="q_raw")
        nc.sync.dma_start(q_raw[:], query.rearrange("(p j) q -> p j q", j=PACK))
        k_words = sb.tile([P, T], U32, name="k_words", tag="keys_then_old")
        keys_i32 = keys_words[0].rearrange("p t r -> p (t r)").bitcast(I32)
        nc.sync.dma_start(k_words[:, :KEYS_FIRST].bitcast(I32), keys_i32[:, :KEYS_FIRST])
        nc.sync.dma_start(offsets[:], offs)
        for r in range(4):
            nc.sync.dma_start(k_bytes[r:P:32, :].bitcast(I32), keys_scales[0, r:16:4, :].bitcast(I32))
        nc.sync.dma_start(k_words[:, KEYS_FIRST:].bitcast(I32), keys_i32[:, KEYS_FIRST:])
        g_raw = sb.tile([P, PACK, Q], F32, name="g_raw")
        nc.sync.dma_start(g_raw[:], gout.rearrange("(p j) q -> p j q", j=PACK))
        mix_exp = sb.tile([P, 1], F32, name="mix_exp")
        nc.sync.dma_start(mix_exp[:], share)
        for r in range(4):
            nc.sync.dma_start(v_bytes[V_PLANE + r : P : 32, :].bitcast(I32), vals_scales[0, r:16:4, :].bitcast(I32))
        v_words = sb.tile([P, T], U32, name="v_words", tag="v_words_then_part_exp")
        nc.sync.dma_start(v_words[:].bitcast(I32), vals_words[0].rearrange("p t r -> p (t r)").bitcast(I32))

        placed = sb.tile([P, T], F32, name="placed")
        nc.vector.memset(placed[:], 0.0)

        pieces = len(KEY_PIECES)
        mixes = sb.tile([P, 2 * pieces], F32, name="mixes")
        mix_sig = mixes[:, pieces : pieces + 1]
        mix_sig_neg = sb.tile([P, 1], F32, name="mix_sig_neg")
        nc.scalar.activation(mixes[:, :pieces], mix_exp[:].to_broadcast([P, pieces]), ACT.Copy)
        nc.scalar.activation(mixes[:, pieces:], mix_exp[:].to_broadcast([P, pieces]), ACT.Copy, bias=3.0, scale=-3.0)
        nc.scalar.activation(mix_sig_neg[:], mix_exp[:], ACT.Copy, bias=-3.0, scale=3.0)

        q_bf = sb.tile([P, Q, PACK], BF16, name="q_bf", align_bytes=64)
        nc.scalar.copy(q_bf[:], q_raw[:].rearrange("p j q -> p q j"))
        ks = sb.tile([P, SLOTS], U8, name="ks", align_bytes=64)
        nc.vector.tensor_copy(ks[:], k_bytes[:].indirect(offsets[:]))
        q_codes = sb.tile([P, Q], U32, name="q_codes", align_bytes=64)
        q_scales = sb.tile([P, Q], U8, name="q_scales", align_bytes=64)
        nc.vector.quantize_mx(out=q_codes[:].bitcast(FP8X4), scales=q_scales[:], in_=q_bf[:].rearrange("p q j -> p (q j)"))

        g_bf = sb.tile([P, Q, PACK], BF16, name="g_bf", align_bytes=64)
        nc.scalar.copy(g_bf[:], g_raw[:].rearrange("p j q -> p q j"))

        e0_lo = sb.tile([P, HALF], F32, name="e0_lo", tag="e0_lo_then_vw", align_bytes=64)
        e0_hi = sb.tile([P, HALF], F32, name="e0_hi")
        s0 = sb.tile([P, SLOTS], F32, name="s0")
        sums = sb.tile([P, 2 * pieces], F32, name="sums")
        kw = sb.tile([P, SLOTS], U32, name="kw", tag="k_bytes_then_kw", align_bytes=64)
        scores = []
        for n, (lo, hi) in enumerate(KEY_PIECES):
            nc.vector.tensor_copy(kw[:, lo:hi], k_words[:].indirect(offsets[:, lo // 16 : hi // 16]))
            a = ps.tile([P, hi - lo], F32, name="a%d" % n)
            nc.tensor.matmul_mx(out=a[:], lhsT=q_codes[:].bitcast(FP8X4), lhsT_scale=q_scales[:], rhs=kw[:, lo:hi].bitcast(FP8X4), rhs_scale=ks[:, lo:hi], start=True, stop=True)
            e0_piece = e0_lo[:, lo:hi] if hi <= HALF else e0_hi[:, lo - HALF : hi - HALF]
            nc.scalar.activation(e0_piece, a[:], ACT.Exp, accum_out=sums[:, n : n + 1])
            scores.append(a)
        for n, (lo, hi) in enumerate(KEY_PIECES):
            nc.scalar.activation(s0[:, lo:hi], scores[n][:], ACT.Sigmoid, accum_out=sums[:, pieces + n : pieces + n + 1])
        s0_sq = sb.tile([P, SLOTS], F32, name="s0_sq")
        for h in range(2):
            nc.scalar.activation(s0_sq[:, h * HALF : (h + 1) * HALF], s0[:, h * HALF : (h + 1) * HALF], ACT.Square)

        result = sb.tile([P, T], F32, name="result", tag="keys_then_old")
        nc.sync.dma_start(result[:], old)

        vs = sb.tile([P, SLOTS], U8, name="vs", align_bytes=64)
        nc.vector.tensor_copy(vs[:], v_bytes[:].indirect(offsets[:]))
        g_codes = sb.tile([P, Q], U32, name="g_codes", align_bytes=64)
        g_scales = sb.tile([P, Q], U8, name="g_scales", align_bytes=64)
        nc.vector.quantize_mx(out=g_codes[:].bitcast(FP8X4), scales=g_scales[:], in_=g_bf[:].rearrange("p q j -> p (q j)"))
        part_exp_lo = sb.tile([P, HALF], F32, name="part_exp_lo", tag="v_bytes_then_part_exp_lo", align_bytes=64)
        nc.vector.tensor_scalar(part_exp_lo[:], e0_lo[:], mix_exp[:], None, ALU.mult)
        vw = sb.tile([P, SLOTS], U32, name="vw", tag="e0_lo_then_vw", align_bytes=64)
        nc.vector.tensor_copy(vw[:], v_words[:].indirect(offsets[:]))
        c0 = ps.tile([P, SLOTS], F32, name="c0")
        nc.tensor.matmul_mx(out=c0[:], lhsT=g_codes[:].bitcast(FP8X4), lhsT_scale=g_scales[:], rhs=vw[:].bitcast(FP8X4), rhs_scale=vs[V_PLANE:, :], start=True, stop=True)

        lo_half, hi_half = slice(0, HALF), slice(HALF, SLOTS)
        late = sb.tile([P, SLOTS + HALF + 2 * pieces], F32, name="late", tag="v_words_then_part_exp")
        part, part_exp_hi, mixed_sums = late[:, :SLOTS], late[:, SLOTS : SLOTS + HALF], late[:, SLOTS + HALF :]
        nc.vector.tensor_scalar(part_exp_hi, e0_hi[:], mix_exp[:], None, ALU.mult)

        slope = sb.tile([P, SLOTS], F32, name="slope")
        z = sb.tile([P, 1], F32, name="z")
        rz = sb.tile([P, 1], F32, name="rz")
        nc.vector.scalar_tensor_tensor(part[:, lo_half], s0[:, lo_half], mix_sig, part_exp_lo[:], ALU.mult, ALU.add)
        nc.vector.scalar_tensor_tensor(mixed_sums, sums[:], 1.0, mixes[:], ALU.mult, ALU.mult, accum_out=z[:])
        nc.vector.scalar_tensor_tensor(part[:, hi_half], s0[:, hi_half], mix_sig, part_exp_hi, ALU.mult, ALU.add)
        nc.vector.reciprocal(rz[:], z[:])
        nc.vector.scalar_tensor_tensor(slope[:, lo_half], s0_sq[:, lo_half], mix_sig_neg[:], part[:, lo_half], ALU.mult, ALU.add)
        rz512 = sb.tile([P, 1], F32, name="rz512")
        nc.scalar.activation(rz512[:], rz[:], ACT.Copy, scale=512.0)
        weighted = sb.tile([P, SLOTS], F32, name="weighted")
        mean = sb.tile([P, 1], F32, name="mean")
        nc.vector.scalar_tensor_tensor(weighted[:], c0[:], rz[:], part, ALU.mult, ALU.mult, accum_out=mean[:])
        nc.vector.scalar_tensor_tensor(slope[:, hi_half], s0_sq[:, hi_half], mix_sig_neg[:], part[:, hi_half], ALU.mult, ALU.add)
        dp512 = sb.tile([P, SLOTS], F32, name="dp512")
        nc.vector.tensor_scalar(dp512[:], c0[:], mean[:], rz512[:], ALU.subtract, ALU.mult)
        nc.vector.tensor_tensor(placed[:].indirect(offsets[:]), dp512[:], slope[:], ALU.mult)

        for lo, hi in zip(OUT_EDGES[:-1], OUT_EDGES[1:]):
            cols = slice(lo, hi)
            nc.vector.tensor_tensor(result[:, cols], result[:, cols], placed[:, cols], ALU.add)
            nc.sync.dma_start(out[:, cols], result[:, cols])
